import numpy as np
import ml_dtypes

BF16 = ml_dtypes.bfloat16


def bf(x):
    return np.asarray(x, np.float32).astype(BF16)


def f32(x):
    return np.asarray(x, np.float32)


def f64(x):
    return np.asarray(x).astype(np.float64)


def striped(idx):
    return np.concatenate([l.reshape(-1, 16).T for l in idx])


def rows(idx, k):
    return np.tile(np.repeat(idx, 16, axis=0), (k // (16 * 8), 1))


def look(tab, idx):
    return np.take_along_axis(f64(tab), rows(idx, len(tab)), axis=1)


K, S, D, V, N = 128, 2048, 4, 512, 2048


def setup_inputs():
    return {"tab": f32(np.random.standard_normal((K, S))), "u": f32(np.random.uniform(0.2, 1.0, (D, K, V))), "offs": striped(np.stack([np.random.permutation(S)[:N] for _ in range(8)]))}


def reference(tab, u, offs):
    idx = np.stack([g.T.reshape(-1) for g in np.split(offs, 8)])
    x = sum(f64(u[d]) * look(tab, idx[:, d * V:(d + 1) * V]) for d in range(D))
    return x

@@ -1,0 +1,35 @@
+import concourse.mybir as mybir
+
+F32, U16 = mybir.dt.float32, mybir.dt.uint16
+MULT, ADD = mybir.AluOpType.mult, mybir.AluOpType.add
+
+
+def tile_lookup_mix_mul_out_kernel(tc, tab, u, offs, out):
+    nc = tc.nc
+    rows, table_columns = tab.shape
+    places, weight_rows, columns = u.shape
+    list_columns = columns // 16
+
+    with tc.tile_pool(name="held", bufs=1) as held:
+        lists = held.tile([rows, places * list_columns], U16)
+        table = held.tile([rows, table_columns], F32)
+        nc.sync.dma_start(lists[:], offs)
+        nc.sync.dma_start(table[:], tab)
+        weights = []
+        for d in range(places):
+            weight = held.tile([rows, columns], F32, name=f"weight{d}")
+            nc.sync.dma_start(weight[:], u[d])
+            weights.append(weight)
+
+        total = None
+        for d in range(places):
+            product = held.tile([rows, columns], F32, name=f"product{d}")
+            picked = table[:].indirect(lists[:, d * list_columns : (d + 1) * list_columns])
+            nc.vector.tensor_tensor(product[:], picked, weights[d][:], MULT)
+            if total is None:
+                total = product
+            else:
+                longer = held.tile([rows, columns], F32, name=f"total{d}")
+                nc.vector.tensor_tensor(longer[:], total[:], product[:], ADD)
+                total = longer
+        nc.sync.dma_start(out, total[:])

@@ -1,35 +1,57 @@
 import concourse.mybir as mybir
+from concourse.masks import make_identity
 
 F32, U16 = mybir.dt.float32, mybir.dt.uint16
 MULT, ADD = mybir.AluOpType.mult, mybir.AluOpType.add
+
+FLOPS = 2 * 4 * 128 * 512
 
 
 def tile_lookup_mix_mul_out_kernel(tc, tab, u, offs, out):
     nc = tc.nc
     rows, table_columns = tab.shape
     places, weight_rows, columns = u.shape
-    list_columns = columns // 16
+    half = columns // 2
 
-    with tc.tile_pool(name="held", bufs=1) as held:
-        lists = held.tile([rows, places * list_columns], U16)
+    with (
+        tc.tile_pool(name="held", bufs=1) as held,
+        tc.psum_pool(name="sums", bufs=1) as sums,
+    ):
+        lists = held.tile([rows, places * columns // 16], U16)
         table = held.tile([rows, table_columns], F32)
         nc.sync.dma_start(lists[:], offs)
         nc.sync.dma_start(table[:], tab)
-        weights = []
-        for d in range(places):
-            weight = held.tile([rows, columns], F32, name=f"weight{d}")
-            nc.sync.dma_start(weight[:], u[d])
-            weights.append(weight)
 
-        total = None
+        weights = {}
+        for left in (0, half):
+            for d in range(places):
+                weight = held.tile([rows, half], F32, name=f"weight{d}_{left}")
+                nc.sync.dma_start(weight[:], u[d, :, left : left + half])
+                weights[left, d] = weight
+
+        identity = held.tile([rows, rows], F32)
+        make_identity(nc, identity[:])
+
+        def weighted_look_up(left, d):
+            product = held.tile([rows, half], F32, name=f"product{d}_{left}")
+            start = (d * columns + left) // 16
+            picked = table[:].indirect(lists[:, start : start + half // 16])
+            nc.vector.tensor_tensor(product[:], picked, weights[left, d][:], MULT)
+            return product
+
+        left_sum = sums.tile([rows, half], F32)
         for d in range(places):
-            product = held.tile([rows, columns], F32, name=f"product{d}")
-            picked = table[:].indirect(lists[:, d * list_columns : (d + 1) * list_columns])
-            nc.vector.tensor_tensor(product[:], picked, weights[d][:], MULT)
-            if total is None:
-                total = product
-            else:
-                longer = held.tile([rows, columns], F32, name=f"total{d}")
-                nc.vector.tensor_tensor(longer[:], total[:], product[:], ADD)
-                total = longer
-        nc.sync.dma_start(out, total[:])
+            product = weighted_look_up(0, d)
+            nc.tensor.matmul(left_sum[:], identity[:], product[:], start=(d == 0), stop=(d == places - 1))
+        left_out = held.tile([rows, half], F32)
+        nc.scalar.copy(left_out[:], left_sum[:])
+        nc.scalar.dma_start(out[:, 0:half], left_out[:])
+
+        right_sum = sums.tile([rows, half], F32)
+        for d in range(places - 1):
+            product = weighted_look_up(half, d)
+            nc.tensor.matmul(right_sum[:], identity[:], product[:], start=(d == 0), stop=(d == places - 2))
+        last_product = weighted_look_up(half, places - 1)
+        right_out = held.tile([rows, half], F32)
+        nc.vector.tensor_tensor(right_out[:], last_product[:], right_sum[:], ADD)
+        nc.sync.dma_start(out[:, half:columns], right_out[:])

@@ -1,8 +1,11 @@
 import concourse.mybir as mybir
 from concourse.masks import make_identity
 
-F32, U16 = mybir.dt.float32, mybir.dt.uint16
+F32, BF16, U16 = mybir.dt.float32, mybir.dt.bfloat16, mybir.dt.uint16
 MULT, ADD = mybir.AluOpType.mult, mybir.AluOpType.add
+
+BANK = 512
+WARM_UPS = 10
 
 FLOPS = 2 * 4 * 128 * 512
 
@@ -28,6 +31,12 @@ def tile_lookup_mix_mul_out_kernel(tc, tab, u, offs, out):
                 weight = held.tile([rows, half], F32, name=f"weight{d}_{left}")
                 nc.sync.dma_start(weight[:], u[d, :, left : left + half])
                 weights[left, d] = weight
+
+        zeros = held.tile([rows, BANK], BF16)
+        nc.vector.memset(zeros[:], 0.0)
+        unused = sums.tile([rows, BANK], F32)
+        for warm_up in range(WARM_UPS):
+            nc.tensor.matmul(unused[:], zeros[:, 0:rows], zeros[:], start=True, stop=True)
 
         identity = held.tile([rows, rows], F32)
         make_identity(nc, identity[:])

import concourse.mybir as mybir
from concourse.masks import make_identity

F32, BF16, U16 = mybir.dt.float32, mybir.dt.bfloat16, mybir.dt.uint16
MULT, ADD = mybir.AluOpType.mult, mybir.AluOpType.add

BANK = 512
WARM_UPS = 10

FLOPS = 2 * 4 * 128 * 512


def tile_lookup_mix_mul_out_kernel(tc, tab, u, offs, out):
    nc = tc.nc
    rows, table_columns = tab.shape
    places, weight_rows, columns = u.shape
    half = columns // 2

    with (
        tc.tile_pool(name="held", bufs=1) as held,
        tc.psum_pool(name="sums", bufs=1) as sums,
    ):
        lists = held.tile([rows, places * columns // 16], U16)
        table = held.tile([rows, table_columns], F32)
        nc.sync.dma_start(lists[:], offs)
        nc.sync.dma_start(table[:], tab)

        weights = {}
        for left in (0, half):
            for d in range(places):
                weight = held.tile([rows, half], F32, name=f"weight{d}_{left}")
                nc.sync.dma_start(weight[:], u[d, :, left : left + half])
                weights[left, d] = weight

        zeros = held.tile([rows, BANK], BF16)
        nc.vector.memset(zeros[:], 0.0)
        unused = sums.tile([rows, BANK], F32)
        for warm_up in range(WARM_UPS):
            nc.tensor.matmul(unused[:], zeros[:, 0:rows], zeros[:], start=True, stop=True)

        identity = held.tile([rows, rows], F32)
        make_identity(nc, identity[:])

        def weighted_look_up(left, d):
            product = held.tile([rows, half], F32, name=f"product{d}_{left}")
            start = (d * columns + left) // 16
            picked = table[:].indirect(lists[:, start : start + half // 16])
            nc.vector.tensor_tensor(product[:], picked, weights[left, d][:], MULT)
            return product

        left_sum = sums.tile([rows, half], F32)
        for d in range(places):
            product = weighted_look_up(0, d)
            nc.tensor.matmul(left_sum[:], identity[:], product[:], start=(d == 0), stop=(d == places - 1))
        left_out = held.tile([rows, half], F32)
        nc.scalar.copy(left_out[:], left_sum[:])
        nc.scalar.dma_start(out[:, 0:half], left_out[:])

        right_sum = sums.tile([rows, half], F32)
        for d in range(places - 1):
            product = weighted_look_up(half, d)
            nc.tensor.matmul(right_sum[:], identity[:], product[:], start=(d == 0), stop=(d == places - 2))
        last_product = weighted_look_up(half, places - 1)
        right_out = held.tile([rows, half], F32)
        nc.vector.tensor_tensor(right_out[:], last_product[:], right_sum[:], ADD)
        nc.sync.dma_start(out[:, half:columns], right_out[:])
